import numpy as np
import ml_dtypes


def mxq(x, axis, fmt="e4m3"):
    dtype, down = {"e4m3": (ml_dtypes.float8_e4m3fn, 7), "e5m2": (ml_dtypes.float8_e5m2, 14)}[fmt]
    v = np.moveaxis(np.asarray(x, np.float32).astype(ml_dtypes.bfloat16).astype(np.float64), axis, -1)
    blocks = v.reshape(v.shape[:-1] + (-1, 32))
    amax = np.abs(blocks).max(-1, keepdims=True)
    byte = np.maximum(np.where(amax > 0, np.frexp(amax)[1] - 1 + 127, 0) - down, 1)
    scale = np.exp2(byte - 127.0)
    codes = (blocks / scale).astype(np.float32).astype(dtype).astype(np.float64)
    return np.moveaxis((codes * scale).reshape(v.shape), -1, axis)


WIDE = False


def mx_kscale(k):
    if not WIDE:
        return np.ones(k)
    levels = np.array([30, -30])
    if k % 512:
        return np.exp2(np.random.permutation(np.resize(levels, k // 32))).repeat(32)
    a = np.empty((k // 512, 16))
    for p in range(k // 512):
        a[p, :8] = np.random.permutation(np.resize(levels, 8))
        for g in range(8):
            far = levels[np.abs(levels - a[p, g]) >= 10]
            a[p, g + 8] = far[np.random.randint(len(far))]
    return np.exp2(a.ravel()).repeat(32)


def f64(x):
    return np.asarray(x).astype(np.float64)


def striped(idx):
    return np.tile(np.asarray(idx).reshape(-1, 16).T, (8, 1)).astype(np.uint16)


def unstriped(offs):
    return offs[:16].T.reshape(-1).astype(np.int64)


def striped8(idx):
    return np.asarray(idx).reshape(8, -1, 16).transpose(0, 2, 1).reshape(128, -1).astype(np.uint16)


def unstriped8(offs):
    return offs.reshape(8, 16, -1).transpose(0, 2, 1).reshape(8, -1).astype(np.int64)


def pick8(x, idx, run):
    r = np.arange(len(x))
    return x[r[:, None], idx[r % (8 * run) // run]]


E2M1 = np.array([0.0, 0.5, 1.0, 1.5, 2.0, 3.0, 4.0, 6.0, -0.0, -0.5, -1.0, -1.5, -2.0, -3.0, -4.0, -6.0])


def pack_weight(w, fmt):
    k, n = w.shape
    w = f64(np.asarray(w, np.float32).astype(ml_dtypes.bfloat16)).reshape(k // 32, 32, n)
    amax = np.abs(w).max(1)
    if fmt in ("e4m3", "e5m2"):
        byte = np.frexp(amax)[1] - 1 + 127 - (7 if fmt == "e4m3" else 14)
    else:
        mant, ex = np.frexp(amax / 6.0)
        byte = np.where(mant > 0.5, ex, ex - 1) + 127
    byte = np.clip(np.where(amax > 0, byte, 1), 1, 254)
    scaled = (w * np.exp2(127.0 - byte)[:, None, :]).reshape(k, n).astype(np.float32)
    by_word = np.ascontiguousarray(scaled.reshape(k // 512, 128, 4, n).transpose(0, 1, 3, 2))
    if fmt in ("e4m3", "e5m2"):
        words = by_word.astype(ml_dtypes.float8_e4m3fn if fmt == "e4m3" else ml_dtypes.float8_e5m2).view(np.uint8)
    else:
        c = by_word.astype(ml_dtypes.float4_e2m1fn).view(np.uint8) & 0xF
        words = (c[..., 0::2] | (c[..., 1::2] << 4)).reshape(k // 512, 128, 2 * n)
    return np.ascontiguousarray(words), np.ascontiguousarray(byte.astype(np.uint8).reshape(k // 512, 16, n))


def unpack_weight(words, scales, fmt):
    g, _, n = scales.shape
    words = np.ascontiguousarray(words).reshape(g, 128, n, -1)
    if fmt in ("e4m3", "e5m2"):
        vals = words.view(ml_dtypes.float8_e4m3fn if fmt == "e4m3" else ml_dtypes.float8_e5m2).astype(np.float64)
    else:
        nib = np.empty((g, 128, n, 4), np.uint8)
        nib[..., 0::2] = words & 0xF
        nib[..., 1::2] = words >> 4
        vals = E2M1[nib]
    vals = vals * np.repeat(np.exp2(scales.astype(np.float64) - 127.0), 8, axis=1)[..., None]
    return vals.transpose(0, 1, 3, 2).reshape(g * 512, n)


K, T, J, R, F, Z, C, O, N, E = 512, 1024, 256, 512, 512, 1024, 512, 128, 256, 512


def setup_inputs():
    n = np.random.standard_normal
    idx = np.random.permutation(T)[:J]
    idx2 = np.random.permutation(Z)[:J]
    idx3 = np.stack([np.random.permutation(C)[:J] for _ in range(8)])
    idx4 = np.random.permutation(C)[:O]
    idx5 = np.random.permutation(J)[:O]
    idx6 = np.random.permutation(E)[:O]
    idx7 = np.random.permutation(E)[:O]
    fk = mx_kscale(K)
    ff = mx_kscale(F)
    fr = mx_kscale(R)
    xtp = pack_weight(n((K, T)) / fk[:, None], "e5m2")
    xop = pack_weight(n((F, Z)) / ff[:, None], "e4m3")
    wp = pack_weight(n((K, R)) * 1 / np.sqrt(K) * fk[:, None] * fr, "e2m1")
    w2p = pack_weight(n((K, R)) * 1 / np.sqrt(K) * fk[:, None], "e4m3")
    w0p = pack_weight(n((F, R)) * 1 / np.sqrt(F) * ff[:, None], "e4m3")
    wbp = pack_weight(n((R, N)) * 1 / np.sqrt(R) / fr[:, None], "e2m1")
    return {
        "xt_words": xtp[0],
        "xt_scales": xtp[1],
        "xo_words": xop[0],
        "xo_scales": xop[1],
        "w_words": wp[0],
        "w_scales": wp[1],
        "w2_words": w2p[0],
        "w2_scales": w2p[1],
        "w0_words": w0p[0],
        "w0_scales": w0p[1],
        "wb_words": wbp[0],
        "wb_scales": wbp[1],
        "offs": striped(idx),
        "offs2": striped(idx2),
        "offs3": striped8(idx3),
        "offs4": striped(idx4),
        "offs5": striped(idx5),
        "offs6": striped(idx6),
        "offs7": striped(idx7),
    }


def reference(xt_words, xt_scales, xo_words, xo_scales, w_words, w_scales, w2_words, w2_scales, w0_words, w0_scales, wb_words, wb_scales, offs, offs2, offs3, offs4, offs5, offs6, offs7):
    idx = unstriped(offs)
    idx2 = unstriped(offs2)
    idx3 = unstriped8(offs3)
    idx4 = unstriped(offs4)
    idx5 = unstriped(offs5)
    idx6 = unstriped(offs6)
    idx7 = unstriped(offs7)
    xtu = unpack_weight(xt_words, xt_scales, "e5m2")
    xou = unpack_weight(xo_words, xo_scales, "e4m3")
    wu = unpack_weight(w_words, w_scales, "e2m1")
    w2u = unpack_weight(w2_words, w2_scales, "e4m3")
    w0u = unpack_weight(w0_words, w0_scales, "e4m3")
    wbu = unpack_weight(wb_words, wb_scales, "e2m1")
    xtidxg = xtu[:, idx]
    a = wu.T @ xtidxg
    xoidx2g = xou[:, idx2]
    b = w2u.T @ xtidxg + w0u.T @ xoidx2g
    lb = b[:, 0:1]
    la = a[:, 0:1]
    pw = np.zeros((R, C))
    pw[np.arange(R)[:, None], idx3[np.arange(R) % 512 // 64]] = a
    hid = np.maximum(pw[:, idx4] * lb, b[:, idx5] * la)
    hidq = mxq(hid, 0, "e4m3")
    p = wbu.T @ hidq
    pa = np.zeros((N, E))
    pa[:, idx6] = p
    pb = np.zeros((N, E))
    pb[:, idx7] = p
    y = pa + pb
    return y

@@ -1,0 +1,194 @@
+from contextlib import ExitStack
+
+import concourse.mybir as mybir
+
+K, T, J, R, C, O, N, E = 512, 1024, 256, 512, 512, 128, 256, 512
+FLOPS = 2 * K * R * J * 3 + 2 * R * N * O
+
+F32 = mybir.dt.float32
+BF16 = mybir.dt.bfloat16
+I32 = mybir.dt.int32
+U32 = mybir.dt.uint32
+U16 = mybir.dt.uint16
+U8 = mybir.dt.uint8
+E4M3 = mybir.dt.float8_e4m3fn_x4
+E5M2 = mybir.dt.float8_e5m2_x4
+E2M1 = mybir.dt.float4_e2m1fn_x4
+COPY = mybir.ActivationFunctionType.Copy
+
+P = 128
+PACK = 4
+HALF = J // 2
+
+
+def tile_list_ownlead_leaned_one_pagetwice_kernel(
+    tc, xt_words, xt_scales, xo_words, xo_scales, w_words, w_scales, w2_words, w2_scales,
+    w0_words, w0_scales, wb_words, wb_scales, offs, offs2, offs3, offs4, offs5, offs6, offs7, out,
+):
+    nc = tc.nc
+    with ExitStack() as ctx:
+        sb = ctx.enter_context(tc.tile_pool(name="sb", bufs=1))
+        ps = ctx.enter_context(tc.psum_pool(name="ps", bufs=1))
+
+        def tile(name, width, dtype, tag=None):
+            return sb.tile([P, width], dtype, name=name, tag=tag or name, align_bytes=64)
+
+        def load_list(name, src):
+            lst = sb.tile(list(src.shape), U16, name=name)
+            nc.sync.dma_start(lst[:], src)
+            return lst
+
+        def load_words(queue, name, src, width):
+            words = tile(name, width, U32)
+            queue.dma_start(words[:].bitcast(I32), src[0].rearrange("p n t -> p (n t)").bitcast(I32))
+            return words
+
+        def zero_plane(name, width):
+            plane = tile(name, width, U8)
+            nc.vector.memset(plane[:].bitcast(I32), 0)
+            return plane
+
+        def load_plane(queue, plane, src):
+            for q in range(4):
+                queue.dma_start(plane[32 * q : 32 * q + 4, :].bitcast(I32), src[0, 4 * q : 4 * q + 4, :].bitcast(I32))
+
+        def deal(copy, dst, src, t0, t1):
+            copy(
+                out=dst[:, P * t0 : P * t1].rearrange("p (t m) -> p m t", m=P),
+                in_=src.rearrange("p (m t) -> p m t", t=PACK)[:, :, t0:t1],
+            )
+
+        xt_plane = zero_plane("xt_plane", T)
+        w_plane = zero_plane("w_plane", R)
+        w_rows = sb.tile([4, 4, R // 4], I32, name="w_rows")
+        nc.sync.dma_start(w_rows[:], w_scales[0].bitcast(I32).rearrange("(q r) c -> r q c", r=4))
+        idx = load_list("idx", offs)
+        xt_win = load_words(nc.sync, "xt_win", xt_words, T)
+        load_plane(nc.sync, xt_plane, xt_scales)
+        w_raw = tile("w_raw", R, U16)
+        nc.sync.dma_start(w_raw[:].bitcast(I32), w_words[0].bitcast(I32))
+        idx3 = load_list("idx3", offs3)
+
+        w2_plane = zero_plane("w2_plane", R)
+        w0_plane = zero_plane("w0_plane", R)
+        xo_plane = zero_plane("xo_plane", T)
+        wb_plane = zero_plane("wb_plane", N)
+        w2_raw = load_words(nc.sync, "w2_raw", w2_words, R)
+        load_plane(nc.sync, w2_plane, w2_scales)
+        w0_raw = load_words(nc.sync, "w0_raw", w0_words, R)
+        load_plane(nc.sync, w0_plane, w0_scales)
+        idx2 = load_list("idx2", offs2)
+        load_plane(nc.sync, xo_plane, xo_scales)
+        xo_win = load_words(nc.sync, "xo_win", xo_words, T)
+        idx4 = load_list("idx4", offs4)
+        idx5 = load_list("idx5", offs5)
+        wb_codes = tile("wb_codes", N, U16)
+        nc.sync.dma_start(wb_codes[:].bitcast(I32), wb_words[0].bitcast(I32))
+        load_plane(nc.sync, wb_plane, wb_scales)
+        idx6 = load_list("idx6", offs6)
+        idx7 = load_list("idx7", offs7)
+
+        boards = []
+        for t in range(PACK):
+            board = tile("board%d" % t, C, F32)
+            nc.gpsimd.memset(board[:], 0.0)
+            boards.append(board)
+
+        xt_g = tile("xt_g", J, U32)
+        xt_gs = tile("xt_gs", J, U8)
+        w_codes = tile("w_codes", R, U16)
+        w_sc = tile("w_sc", R, U8)
+        a_sb = [tile("a%d" % t, J, F32) for t in range(PACK)]
+        halves = [slice(0, HALF), slice(HALF, J)]
+        cols = [slice(0, HALF // 16), slice(HALF // 16, J // 16)]
+
+        def a_pass(acc, t, js):
+            nc.tensor.matmul_mx(
+                out=acc, lhsT=w_codes[:, P * t : P * (t + 1)].bitcast(E2M1), lhsT_scale=w_sc[:, P * t : P * (t + 1)],
+                rhs=xt_g[:, js].bitcast(E5M2), rhs_scale=xt_gs[:, js], start=True, stop=True,
+            )
+
+        for q in range(4):
+            nc.vector.tensor_copy(w_plane[32 * q : 32 * q + 4, :].bitcast(I32), w_rows[:, q, :])
+        deal(nc.vector.tensor_copy, w_sc, w_plane[:], 0, 1)
+        deal(nc.scalar.copy, w_codes, w_raw[:], 0, 1)
+        nc.vector.tensor_copy(xt_g[:, halves[0]], xt_win[:].indirect(idx[:, cols[0]]))
+        nc.vector.tensor_copy(xt_gs[:, halves[0]], xt_plane[:].indirect(idx[:, cols[0]]))
+        first = ps.tile([P, HALF], F32, name="first", tag="bank0")
+        a_pass(first[:], 0, halves[0])
+        deal(nc.scalar.copy, w_codes, w_raw[:], 1, PACK)
+        nc.scalar.copy(a_sb[0][:, halves[0]], first[:])
+        nc.scalar.activation(boards[0][:].indirect(idx3[:, cols[0]]), a_sb[0][:, halves[0]], COPY)
+
+        nc.vector.tensor_copy(xt_gs[:, halves[1]], xt_plane[:].indirect(idx[:, cols[1]]))
+        nc.vector.tensor_copy(xt_g[:, halves[1]], xt_win[:].indirect(idx[:, cols[1]]))
+        second = ps.tile([P, HALF], F32, name="second", tag="bank1")
+        a_pass(second[:], 0, halves[1])
+        deal(nc.vector.tensor_copy, w_sc, w_plane[:], 1, PACK)
+        nc.vector.tensor_copy(a_sb[0][:, halves[1]], second[:])
+        nc.scalar.activation(boards[0][:].indirect(idx3[:, cols[1]]), a_sb[0][:, halves[1]], COPY)
+        for t in range(1, PACK):
+            acc = ps.tile([P, J], F32, name="acc_a%d" % t, tag="bank%d" % (t + 1))
+            a_pass(acc[:], t, slice(0, J))
+            nc.vector.tensor_copy(a_sb[t][:], acc[:])
+            nc.scalar.activation(boards[t][:].indirect(idx3[:]), a_sb[t][:], COPY)
+
+        w2_codes = tile("w2_codes", R, U32)
+        w2_sc = tile("w2_sc", R, U8)
+        w0_codes = tile("w0_codes", R, U32)
+        w0_sc = tile("w0_sc", R, U8)
+        xo_g = tile("xo_g", J, U32)
+        xo_gs = tile("xo_gs", J, U8)
+        deal(nc.vector.tensor_copy, w2_codes[:].bitcast(I32), w2_raw[:].bitcast(I32), 0, PACK)
+        deal(nc.vector.tensor_copy, w2_sc, w2_plane[:], 0, PACK)
+        deal(nc.vector.tensor_copy, w0_codes[:].bitcast(I32), w0_raw[:].bitcast(I32), 0, PACK)
+        deal(nc.vector.tensor_copy, w0_sc, w0_plane[:], 0, PACK)
+        nc.vector.tensor_copy(xo_gs[:], xo_plane[:].indirect(idx2[:]))
+        nc.vector.tensor_copy(xo_g[:], xo_win[:].indirect(idx2[:]))
+
+        hid = tile("hid", O * PACK, BF16)
+        for t in range(PACK):
+            ms = slice(P * t, P * (t + 1))
+            acc = ps.tile([P, J], F32, name="acc_b%d" % t, tag="bank%d" % ((t + 5) % 8))
+            nc.tensor.matmul_mx(
+                out=acc[:], lhsT=w2_codes[:, ms].bitcast(E4M3), lhsT_scale=w2_sc[:, ms],
+                rhs=xt_g[:].bitcast(E5M2), rhs_scale=xt_gs[:], start=True, stop=False,
+            )
+            nc.tensor.matmul_mx(
+                out=acc[:], lhsT=w0_codes[:, ms].bitcast(E4M3), lhsT_scale=w0_sc[:, ms],
+                rhs=xo_g[:].bitcast(E4M3), rhs_scale=xo_gs[:], start=False, stop=True,
+            )
+            b_sb = tile("b%d" % t, J, F32)
+            nc.vector.tensor_copy(b_sb[:], acc[:])
+            from_b = tile("from_b%d" % t, O, F32)
+            from_board = tile("from_board%d" % t, O, F32)
+            nc.scalar.activation(from_b[:], b_sb[:].indirect(idx5[:]), COPY, scale=a_sb[t][:, 0:1])
+            nc.scalar.activation(from_board[:], boards[t][:].indirect(idx4[:]), COPY, scale=b_sb[:, 0:1])
+            nc.vector.tensor_max(hid[:, t::PACK], from_board[:], from_b[:])
+
+        hid_codes = tile("hid_codes", O, U32)
+        hid_sc = tile("hid_sc", O, U8)
+        nc.vector.quantize_mx(out=hid_codes[:].bitcast(E4M3), scales=hid_sc[:], in_=hid[:])
+        pages = []
+        for name, tag in (("pa0", "w2_raw"), ("pb0", "w0_raw"), ("pa1", "w2_codes"), ("pb1", "w0_codes")):
+            page = tile(name, E, F32, tag=tag)
+            nc.gpsimd.memset(page[:], 0.0)
+            pages.append(page)
+        p_sb = []
+        for h, copy in ((0, nc.vector.tensor_copy), (1, nc.scalar.copy)):
+            ns = slice(P * h, P * (h + 1))
+            acc = ps.tile([P, O], F32, name="acc_p%d" % h, tag="bank%d" % (h + 1))
+            nc.tensor.matmul_mx(
+                out=acc[:], lhsT=wb_codes[:, ns].bitcast(E2M1), lhsT_scale=wb_plane[:, ns],
+                rhs=hid_codes[:].bitcast(E4M3), rhs_scale=hid_sc[:], start=True, stop=True,
+            )
+            p_half = tile("p%d" % h, O, F32)
+            copy(p_half[:], acc[:])
+            p_sb.append(p_half)
+        for h in range(2):
+            pa, pb = pages[2 * h], pages[2 * h + 1]
+            nc.vector.tensor_copy(pa[:].indirect(idx6[:]), p_sb[h][:])
+            nc.scalar.activation(pb[:].indirect(idx7[:]), p_sb[h][:], COPY)
+            y = tile("y%d" % h, E, F32)
+            nc.vector.tensor_add(y[:], pa[:], pb[:])
+            nc.sync.dma_start(out[P * h : P * (h + 1), :], y[:])

@@ -52,6 +52,15 @@ def tile_list_ownlead_leaned_one_pagetwice_kernel(
             for q in range(4):
                 queue.dma_start(plane[32 * q : 32 * q + 4, :].bitcast(I32), src[0, 4 * q : 4 * q + 4, :].bitcast(I32))
 
+        def load_folded(rows, src):
+            by_quadrant = src[0].bitcast(I32).rearrange("(u q r) c -> q r u c", u=2, q=2)
+            for q in range(2):
+                nc.sync.dma_start(rows[32 * q : 32 * q + 4, :].bitcast(I32).rearrange("r (u c) -> r u c", u=2), by_quadrant[q])
+
+        def unfold(rows):
+            nc.vector.tensor_copy(rows[64:128, 0:R].bitcast(I32), rows[0:64, R : 2 * R].bitcast(I32))
+            return rows[:, 0:R]
+
         def deal(copy, dst, src, t0, t1):
             copy(
                 out=dst[:, P * t0 : P * t1].rearrange("p (t m) -> p m t", m=P),
@@ -69,17 +78,17 @@ def tile_list_ownlead_leaned_one_pagetwice_kernel(
         nc.sync.dma_start(w_raw[:].bitcast(I32), w_words[0].bitcast(I32))
         idx3 = load_list("idx3", offs3)
 
-        w2_plane = zero_plane("w2_plane", R)
-        w0_plane = zero_plane("w0_plane", R)
+        w2_rows = zero_plane("w2_rows", 2 * R)
+        w0_rows = zero_plane("w0_rows", 2 * R)
         xo_plane = zero_plane("xo_plane", T)
         wb_plane = zero_plane("wb_plane", N)
         w2_raw = load_words(nc.sync, "w2_raw", w2_words, R)
-        load_plane(nc.sync, w2_plane, w2_scales)
         w0_raw = load_words(nc.sync, "w0_raw", w0_words, R)
-        load_plane(nc.sync, w0_plane, w0_scales)
+        load_folded(w2_rows, w2_scales)
+        load_folded(w0_rows, w0_scales)
+        xo_win = load_words(nc.sync, "xo_win", xo_words, T)
         idx2 = load_list("idx2", offs2)
         load_plane(nc.sync, xo_plane, xo_scales)
-        xo_win = load_words(nc.sync, "xo_win", xo_words, T)
         idx4 = load_list("idx4", offs4)
         idx5 = load_list("idx5", offs5)
         wb_codes = tile("wb_codes", N, U16)
@@ -88,11 +97,7 @@ def tile_list_ownlead_leaned_one_pagetwice_kernel(
         idx6 = load_list("idx6", offs6)
         idx7 = load_list("idx7", offs7)
 
-        boards = []
-        for t in range(PACK):
-            board = tile("board%d" % t, C, F32)
-            nc.gpsimd.memset(board[:], 0.0)
-            boards.append(board)
+        boards = [tile("board%d" % t, C, F32) for t in range(PACK)]
 
         xt_g = tile("xt_g", J, U32)
         xt_gs = tile("xt_gs", J, U8)
@@ -118,6 +123,7 @@ def tile_list_ownlead_leaned_one_pagetwice_kernel(
         a_pass(first[:], 0, halves[0])
         deal(nc.scalar.copy, w_codes, w_raw[:], 1, PACK)
         nc.scalar.copy(a_sb[0][:, halves[0]], first[:])
+        nc.vector.memset(boards[0][:].bitcast(I32), 0)
         nc.scalar.activation(boards[0][:].indirect(idx3[:, cols[0]]), a_sb[0][:, halves[0]], COPY)
 
         nc.vector.tensor_copy(xt_gs[:, halves[1]], xt_plane[:].indirect(idx[:, cols[1]]))
@@ -131,6 +137,7 @@ def tile_list_ownlead_leaned_one_pagetwice_kernel(
             acc = ps.tile([P, J], F32, name="acc_a%d" % t, tag="bank%d" % (t + 1))
             a_pass(acc[:], t, slice(0, J))
             nc.vector.tensor_copy(a_sb[t][:], acc[:])
+            nc.vector.memset(boards[t][:].bitcast(I32), 0)
             nc.scalar.activation(boards[t][:].indirect(idx3[:]), a_sb[t][:], COPY)
 
         w2_codes = tile("w2_codes", R, U32)
@@ -140,11 +147,11 @@ def tile_list_ownlead_leaned_one_pagetwice_kernel(
         xo_g = tile("xo_g", J, U32)
         xo_gs = tile("xo_gs", J, U8)
         deal(nc.vector.tensor_copy, w2_codes[:].bitcast(I32), w2_raw[:].bitcast(I32), 0, PACK)
-        deal(nc.vector.tensor_copy, w2_sc, w2_plane[:], 0, PACK)
         deal(nc.vector.tensor_copy, w0_codes[:].bitcast(I32), w0_raw[:].bitcast(I32), 0, PACK)
-        deal(nc.vector.tensor_copy, w0_sc, w0_plane[:], 0, PACK)
-        nc.vector.tensor_copy(xo_gs[:], xo_plane[:].indirect(idx2[:]))
+        deal(nc.vector.tensor_copy, w2_sc, unfold(w2_rows), 0, PACK)
+        deal(nc.vector.tensor_copy, w0_sc, unfold(w0_rows), 0, PACK)
         nc.vector.tensor_copy(xo_g[:], xo_win[:].indirect(idx2[:]))
+        nc.vector.tensor_copy(xo_gs[:], xo_plane[:].indirect(idx2[:]))
 
         hid = tile("hid", O * PACK, BF16)
         for t in range(PACK):
@@ -170,7 +177,7 @@ def tile_list_ownlead_leaned_one_pagetwice_kernel(
         hid_sc = tile("hid_sc", O, U8)
         nc.vector.quantize_mx(out=hid_codes[:].bitcast(E4M3), scales=hid_sc[:], in_=hid[:])
         pages = []
-        for name, tag in (("pa0", "w2_raw"), ("pb0", "w0_raw"), ("pa1", "w2_codes"), ("pb1", "w0_codes")):
+        for name, tag in (("pa0", "xo_win"), ("pb0", "xo_g"), ("pa1", "w2_codes"), ("pb1", "w0_codes")):
             page = tile(name, E, F32, tag=tag)
             nc.gpsimd.memset(page[:], 0.0)
             pages.append(page)
@@ -190,5 +197,6 @@ def tile_list_ownlead_leaned_one_pagetwice_kernel(
             nc.vector.tensor_copy(pa[:].indirect(idx6[:]), p_sb[h][:])
             nc.scalar.activation(pb[:].indirect(idx7[:]), p_sb[h][:], COPY)
             y = tile("y%d" % h, E, F32)
-            nc.vector.tensor_add(y[:], pa[:], pb[:])
-            nc.sync.dma_start(out[P * h : P * (h + 1), :], y[:])
+            for queue, es in ((nc.sync, slice(0, E // 2)), (nc.scalar, slice(E // 2, E))) if h else ((nc.sync, slice(0, E)),):
+                nc.vector.tensor_add(y[:, es], pa[:, es], pb[:, es])
+                queue.dma_start(out[P * h : P * (h + 1), es], y[:, es])

@@ -69,7 +69,7 @@ def tile_list_ownlead_leaned_one_pagetwice_kernel(
 
         xt_plane = zero_plane("xt_plane", T)
         w_plane = zero_plane("w_plane", R)
-        w_rows = sb.tile([4, 4, R // 4], I32, name="w_rows")
+        w_rows = sb.tile([4, 4, R // 4], I32, name="w_rows", tag="w_rows", align_bytes=64)
         nc.sync.dma_start(w_rows[:], w_scales[0].bitcast(I32).rearrange("(q r) c -> r q c", r=4))
         idx = load_list("idx", offs)
         xt_win = load_words(nc.sync, "xt_win", xt_words, T)
@@ -97,7 +97,6 @@ def tile_list_ownlead_leaned_one_pagetwice_kernel(
         idx6 = load_list("idx6", offs6)
         idx7 = load_list("idx7", offs7)
 
-        boards = [tile("board%d" % t, C, F32) for t in range(PACK)]
 
         xt_g = tile("xt_g", J, U32)
         xt_gs = tile("xt_gs", J, U8)
@@ -113,9 +112,10 @@ def tile_list_ownlead_leaned_one_pagetwice_kernel(
                 rhs=xt_g[:, js].bitcast(E5M2), rhs_scale=xt_gs[:, js], start=True, stop=True,
             )
 
-        for q in range(4):
+        nc.gpsimd.tensor_copy(w_plane[0:4, :].bitcast(I32), w_rows[:, 0, :])
+        for q in range(1, 4):
             nc.vector.tensor_copy(w_plane[32 * q : 32 * q + 4, :].bitcast(I32), w_rows[:, q, :])
-        deal(nc.vector.tensor_copy, w_sc, w_plane[:], 0, 1)
+        deal(nc.gpsimd.tensor_copy, w_sc, w_plane[:], 0, 1)
         deal(nc.scalar.copy, w_codes, w_raw[:], 0, 1)
         nc.vector.tensor_copy(xt_g[:, halves[0]], xt_win[:].indirect(idx[:, cols[0]]))
         nc.vector.tensor_copy(xt_gs[:, halves[0]], xt_plane[:].indirect(idx[:, cols[0]]))
@@ -123,6 +123,7 @@ def tile_list_ownlead_leaned_one_pagetwice_kernel(
         a_pass(first[:], 0, halves[0])
         deal(nc.scalar.copy, w_codes, w_raw[:], 1, PACK)
         nc.scalar.copy(a_sb[0][:, halves[0]], first[:])
+        boards = [tile("board0", C, F32)]
         nc.vector.memset(boards[0][:].bitcast(I32), 0)
         nc.scalar.activation(boards[0][:].indirect(idx3[:, cols[0]]), a_sb[0][:, halves[0]], COPY)
 
@@ -137,7 +138,9 @@ def tile_list_ownlead_leaned_one_pagetwice_kernel(
             acc = ps.tile([P, J], F32, name="acc_a%d" % t, tag="bank%d" % (t + 1))
             a_pass(acc[:], t, slice(0, J))
             nc.vector.tensor_copy(a_sb[t][:], acc[:])
-            nc.vector.memset(boards[t][:].bitcast(I32), 0)
+            engine, tag = ((nc.vector, None), (nc.gpsimd, "w_rows"), (nc.gpsimd, "w_raw"))[t - 1]
+            boards.append(tile("board%d" % t, C, F32, tag=tag))
+            engine.memset(boards[t][:].bitcast(I32), 0)
             nc.scalar.activation(boards[t][:].indirect(idx3[:]), a_sb[t][:], COPY)
 
         w2_codes = tile("w2_codes", R, U32)

@@ -70,12 +70,12 @@ def tile_list_ownlead_leaned_one_pagetwice_kernel(
         xt_plane = zero_plane("xt_plane", T)
         w_plane = zero_plane("w_plane", R)
         w_rows = sb.tile([4, 4, R // 4], I32, name="w_rows", tag="w_rows", align_bytes=64)
-        nc.sync.dma_start(w_rows[:], w_scales[0].bitcast(I32).rearrange("(q r) c -> r q c", r=4))
+        nc.scalar.dma_start(w_rows[:], w_scales[0].bitcast(I32).rearrange("(q r) c -> r q c", r=4))
+        xt_win = load_words(nc.scalar, "xt_win", xt_words, T)
         idx = load_list("idx", offs)
-        xt_win = load_words(nc.sync, "xt_win", xt_words, T)
-        load_plane(nc.sync, xt_plane, xt_scales)
         w_raw = tile("w_raw", R, U16)
         nc.sync.dma_start(w_raw[:].bitcast(I32), w_words[0].bitcast(I32))
+        load_plane(nc.sync, xt_plane, xt_scales)
         idx3 = load_list("idx3", offs3)
 
         w2_rows = zero_plane("w2_rows", 2 * R)
@@ -117,8 +117,8 @@ def tile_list_ownlead_leaned_one_pagetwice_kernel(
             nc.vector.tensor_copy(w_plane[32 * q : 32 * q + 4, :].bitcast(I32), w_rows[:, q, :])
         deal(nc.gpsimd.tensor_copy, w_sc, w_plane[:], 0, 1)
         deal(nc.scalar.copy, w_codes, w_raw[:], 0, 1)
-        nc.vector.tensor_copy(xt_g[:, halves[0]], xt_win[:].indirect(idx[:, cols[0]]))
         nc.vector.tensor_copy(xt_gs[:, halves[0]], xt_plane[:].indirect(idx[:, cols[0]]))
+        nc.vector.tensor_copy(xt_g[:, halves[0]], xt_win[:].indirect(idx[:, cols[0]]))
         first = ps.tile([P, HALF], F32, name="first", tag="bank0")
         a_pass(first[:], 0, halves[0])
         deal(nc.scalar.copy, w_codes, w_raw[:], 1, PACK)

from contextlib import ExitStack

import concourse.mybir as mybir

K, T, J, R, C, O, N, E = 512, 1024, 256, 512, 512, 128, 256, 512
FLOPS = 2 * K * R * J * 3 + 2 * R * N * O

F32 = mybir.dt.float32
BF16 = mybir.dt.bfloat16
I32 = mybir.dt.int32
U32 = mybir.dt.uint32
U16 = mybir.dt.uint16
U8 = mybir.dt.uint8
E4M3 = mybir.dt.float8_e4m3fn_x4
E5M2 = mybir.dt.float8_e5m2_x4
E2M1 = mybir.dt.float4_e2m1fn_x4
COPY = mybir.ActivationFunctionType.Copy

P = 128
PACK = 4
HALF = J // 2


def tile_list_ownlead_leaned_one_pagetwice_kernel(
    tc, xt_words, xt_scales, xo_words, xo_scales, w_words, w_scales, w2_words, w2_scales,
    w0_words, w0_scales, wb_words, wb_scales, offs, offs2, offs3, offs4, offs5, offs6, offs7, out,
):
    nc = tc.nc
    with ExitStack() as ctx:
        sb = ctx.enter_context(tc.tile_pool(name="sb", bufs=1))
        ps = ctx.enter_context(tc.psum_pool(name="ps", bufs=1))

        def tile(name, width, dtype, tag=None):
            return sb.tile([P, width], dtype, name=name, tag=tag or name, align_bytes=64)

        def load_list(name, src):
            lst = sb.tile(list(src.shape), U16, name=name)
            nc.sync.dma_start(lst[:], src)
            return lst

        def load_words(queue, name, src, width):
            words = tile(name, width, U32)
            queue.dma_start(words[:].bitcast(I32), src[0].rearrange("p n t -> p (n t)").bitcast(I32))
            return words

        def zero_plane(name, width):
            plane = tile(name, width, U8)
            nc.vector.memset(plane[:].bitcast(I32), 0)
            return plane

        def load_plane(queue, plane, src):
            for q in range(4):
                queue.dma_start(plane[32 * q : 32 * q + 4, :].bitcast(I32), src[0, 4 * q : 4 * q + 4, :].bitcast(I32))

        def load_folded(rows, src):
            by_quadrant = src[0].bitcast(I32).rearrange("(u q r) c -> q r u c", u=2, q=2)
            for q in range(2):
                nc.sync.dma_start(rows[32 * q : 32 * q + 4, :].bitcast(I32).rearrange("r (u c) -> r u c", u=2), by_quadrant[q])

        def unfold(rows):
            nc.vector.tensor_copy(rows[64:128, 0:R].bitcast(I32), rows[0:64, R : 2 * R].bitcast(I32))
            return rows[:, 0:R]

        def deal(copy, dst, src, t0, t1):
            copy(
                out=dst[:, P * t0 : P * t1].rearrange("p (t m) -> p m t", m=P),
                in_=src.rearrange("p (m t) -> p m t", t=PACK)[:, :, t0:t1],
            )

        xt_plane = zero_plane("xt_plane", T)
        w_plane = zero_plane("w_plane", R)
        w_rows = sb.tile([4, 4, R // 4], I32, name="w_rows", tag="w_rows", align_bytes=64)
        nc.scalar.dma_start(w_rows[:], w_scales[0].bitcast(I32).rearrange("(q r) c -> r q c", r=4))
        xt_win = load_words(nc.scalar, "xt_win", xt_words, T)
        idx = load_list("idx", offs)
        w_raw = tile("w_raw", R, U16)
        nc.sync.dma_start(w_raw[:].bitcast(I32), w_words[0].bitcast(I32))
        load_plane(nc.sync, xt_plane, xt_scales)
        idx3 = load_list("idx3", offs3)

        w2_rows = zero_plane("w2_rows", 2 * R)
        w0_rows = zero_plane("w0_rows", 2 * R)
        xo_plane = zero_plane("xo_plane", T)
        wb_plane = zero_plane("wb_plane", N)
        w2_raw = load_words(nc.sync, "w2_raw", w2_words, R)
        w0_raw = load_words(nc.sync, "w0_raw", w0_words, R)
        load_folded(w2_rows, w2_scales)
        load_folded(w0_rows, w0_scales)
        xo_win = load_words(nc.sync, "xo_win", xo_words, T)
        idx2 = load_list("idx2", offs2)
        load_plane(nc.sync, xo_plane, xo_scales)
        idx4 = load_list("idx4", offs4)
        idx5 = load_list("idx5", offs5)
        wb_codes = tile("wb_codes", N, U16)
        nc.sync.dma_start(wb_codes[:].bitcast(I32), wb_words[0].bitcast(I32))
        load_plane(nc.sync, wb_plane, wb_scales)
        idx6 = load_list("idx6", offs6)
        idx7 = load_list("idx7", offs7)


        xt_g = tile("xt_g", J, U32)
        xt_gs = tile("xt_gs", J, U8)
        w_codes = tile("w_codes", R, U16)
        w_sc = tile("w_sc", R, U8)
        a_sb = [tile("a%d" % t, J, F32) for t in range(PACK)]
        halves = [slice(0, HALF), slice(HALF, J)]
        cols = [slice(0, HALF // 16), slice(HALF // 16, J // 16)]

        def a_pass(acc, t, js):
            nc.tensor.matmul_mx(
                out=acc, lhsT=w_codes[:, P * t : P * (t + 1)].bitcast(E2M1), lhsT_scale=w_sc[:, P * t : P * (t + 1)],
                rhs=xt_g[:, js].bitcast(E5M2), rhs_scale=xt_gs[:, js], start=True, stop=True,
            )

        nc.gpsimd.tensor_copy(w_plane[0:4, :].bitcast(I32), w_rows[:, 0, :])
        for q in range(1, 4):
            nc.vector.tensor_copy(w_plane[32 * q : 32 * q + 4, :].bitcast(I32), w_rows[:, q, :])
        deal(nc.gpsimd.tensor_copy, w_sc, w_plane[:], 0, 1)
        deal(nc.scalar.copy, w_codes, w_raw[:], 0, 1)
        nc.vector.tensor_copy(xt_gs[:, halves[0]], xt_plane[:].indirect(idx[:, cols[0]]))
        nc.vector.tensor_copy(xt_g[:, halves[0]], xt_win[:].indirect(idx[:, cols[0]]))
        first = ps.tile([P, HALF], F32, name="first", tag="bank0")
        a_pass(first[:], 0, halves[0])
        deal(nc.scalar.copy, w_codes, w_raw[:], 1, PACK)
        nc.scalar.copy(a_sb[0][:, halves[0]], first[:])
        boards = [tile("board0", C, F32)]
        nc.vector.memset(boards[0][:].bitcast(I32), 0)
        nc.scalar.activation(boards[0][:].indirect(idx3[:, cols[0]]), a_sb[0][:, halves[0]], COPY)

        nc.vector.tensor_copy(xt_gs[:, halves[1]], xt_plane[:].indirect(idx[:, cols[1]]))
        nc.vector.tensor_copy(xt_g[:, halves[1]], xt_win[:].indirect(idx[:, cols[1]]))
        second = ps.tile([P, HALF], F32, name="second", tag="bank1")
        a_pass(second[:], 0, halves[1])
        deal(nc.vector.tensor_copy, w_sc, w_plane[:], 1, PACK)
        nc.vector.tensor_copy(a_sb[0][:, halves[1]], second[:])
        nc.scalar.activation(boards[0][:].indirect(idx3[:, cols[1]]), a_sb[0][:, halves[1]], COPY)
        for t in range(1, PACK):
            acc = ps.tile([P, J], F32, name="acc_a%d" % t, tag="bank%d" % (t + 1))
            a_pass(acc[:], t, slice(0, J))
            nc.vector.tensor_copy(a_sb[t][:], acc[:])
            engine, tag = ((nc.vector, None), (nc.gpsimd, "w_rows"), (nc.gpsimd, "w_raw"))[t - 1]
            boards.append(tile("board%d" % t, C, F32, tag=tag))
            engine.memset(boards[t][:].bitcast(I32), 0)
            nc.scalar.activation(boards[t][:].indirect(idx3[:]), a_sb[t][:], COPY)

        w2_codes = tile("w2_codes", R, U32)
        w2_sc = tile("w2_sc", R, U8)
        w0_codes = tile("w0_codes", R, U32)
        w0_sc = tile("w0_sc", R, U8)
        xo_g = tile("xo_g", J, U32)
        xo_gs = tile("xo_gs", J, U8)
        deal(nc.vector.tensor_copy, w2_codes[:].bitcast(I32), w2_raw[:].bitcast(I32), 0, PACK)
        deal(nc.vector.tensor_copy, w0_codes[:].bitcast(I32), w0_raw[:].bitcast(I32), 0, PACK)
        deal(nc.vector.tensor_copy, w2_sc, unfold(w2_rows), 0, PACK)
        deal(nc.vector.tensor_copy, w0_sc, unfold(w0_rows), 0, PACK)
        nc.vector.tensor_copy(xo_g[:], xo_win[:].indirect(idx2[:]))
        nc.vector.tensor_copy(xo_gs[:], xo_plane[:].indirect(idx2[:]))

        hid = tile("hid", O * PACK, BF16)
        for t in range(PACK):
            ms = slice(P * t, P * (t + 1))
            acc = ps.tile([P, J], F32, name="acc_b%d" % t, tag="bank%d" % ((t + 5) % 8))
            nc.tensor.matmul_mx(
                out=acc[:], lhsT=w2_codes[:, ms].bitcast(E4M3), lhsT_scale=w2_sc[:, ms],
                rhs=xt_g[:].bitcast(E5M2), rhs_scale=xt_gs[:], start=True, stop=False,
            )
            nc.tensor.matmul_mx(
                out=acc[:], lhsT=w0_codes[:, ms].bitcast(E4M3), lhsT_scale=w0_sc[:, ms],
                rhs=xo_g[:].bitcast(E4M3), rhs_scale=xo_gs[:], start=False, stop=True,
            )
            b_sb = tile("b%d" % t, J, F32)
            nc.vector.tensor_copy(b_sb[:], acc[:])
            from_b = tile("from_b%d" % t, O, F32)
            from_board = tile("from_board%d" % t, O, F32)
            nc.scalar.activation(from_b[:], b_sb[:].indirect(idx5[:]), COPY, scale=a_sb[t][:, 0:1])
            nc.scalar.activation(from_board[:], boards[t][:].indirect(idx4[:]), COPY, scale=b_sb[:, 0:1])
            nc.vector.tensor_max(hid[:, t::PACK], from_board[:], from_b[:])

        hid_codes = tile("hid_codes", O, U32)
        hid_sc = tile("hid_sc", O, U8)
        nc.vector.quantize_mx(out=hid_codes[:].bitcast(E4M3), scales=hid_sc[:], in_=hid[:])
        pages = []
        for name, tag in (("pa0", "xo_win"), ("pb0", "xo_g"), ("pa1", "w2_codes"), ("pb1", "w0_codes")):
            page = tile(name, E, F32, tag=tag)
            nc.gpsimd.memset(page[:], 0.0)
            pages.append(page)
        p_sb = []
        for h, copy in ((0, nc.vector.tensor_copy), (1, nc.scalar.copy)):
            ns = slice(P * h, P * (h + 1))
            acc = ps.tile([P, O], F32, name="acc_p%d" % h, tag="bank%d" % (h + 1))
            nc.tensor.matmul_mx(
                out=acc[:], lhsT=wb_codes[:, ns].bitcast(E2M1), lhsT_scale=wb_plane[:, ns],
                rhs=hid_codes[:].bitcast(E4M3), rhs_scale=hid_sc[:], start=True, stop=True,
            )
            p_half = tile("p%d" % h, O, F32)
            copy(p_half[:], acc[:])
            p_sb.append(p_half)
        for h in range(2):
            pa, pb = pages[2 * h], pages[2 * h + 1]
            nc.vector.tensor_copy(pa[:].indirect(idx6[:]), p_sb[h][:])
            nc.scalar.activation(pb[:].indirect(idx7[:]), p_sb[h][:], COPY)
            y = tile("y%d" % h, E, F32)
            for queue, es in ((nc.sync, slice(0, E // 2)), (nc.scalar, slice(E // 2, E))) if h else ((nc.sync, slice(0, E)),):
                nc.vector.tensor_add(y[:, es], pa[:, es], pb[:, es])
                queue.dma_start(out[P * h : P * (h + 1), es], y[:, es])
